import numpy as np
import ml_dtypes

BF16 = ml_dtypes.bfloat16


def bf(x):
    return np.asarray(x, np.float32).astype(BF16)


def f32(x):
    return np.asarray(x, np.float32)


def f64(x):
    return np.asarray(x).astype(np.float64)


def striped(idx):
    return np.tile(idx.reshape(-1, 16).T, (8, 1))


S, K, M, N, E, Q = 256, 128, 128, 256, 4, 64


def setup_inputs():
    return {"base": bf(np.random.standard_normal((M, S))), "x": bf(np.random.standard_normal((K, N))), "w": bf(np.random.standard_normal((E, K, M)) / np.sqrt(K)), "b": f32(0.5 * np.random.standard_normal((M, 1))), "offs": striped(np.random.permutation(S))}


def reference(base, x, w, b, offs):
    idx = offs[:16].T.reshape(-1)
    z = f64(base).copy()
    for e in range(E):
        z[:, idx[e * Q : (e + 1) * Q]] += f64(w)[e].T @ f64(x)[:, e * Q : (e + 1) * Q]
    return np.maximum(z + f64(b), 0.0)

@@ -1,0 +1,50 @@
+import concourse.mybir as mybir
+from concourse.masks import make_identity
+
+P = 128
+TOKENS = 256
+EXPERTS = 4
+PIECE = 64
+PIECE_COLS = PIECE // 16
+
+BF16, F32, U16 = mybir.dt.bfloat16, mybir.dt.float32, mybir.dt.uint16
+ADD, MAX = mybir.AluOpType.add, mybir.AluOpType.max
+
+FLOPS = 2 * P * P * TOKENS
+
+
+def tile_scatter_matmul_kernel(tc, base, x, w, b, offs, out):
+    nc = tc.nc
+    with (
+        tc.tile_pool(name="held", bufs=1) as held,
+        tc.psum_pool(name="psum", bufs=1) as psum,
+    ):
+        ident = held.tile([P, P], BF16, name="ident")
+        make_identity(nc, ident[:])
+
+        offsets = held.tile([P, TOKENS // 16], U16, name="offsets")
+        nc.sync.dma_start(offsets[:], offs)
+        base_tile = held.tile([P, TOKENS], BF16, name="base_tile")
+        nc.scalar.dma_start(base_tile[:], base)
+        x_tile = held.tile([P, TOKENS], BF16, name="x_tile")
+        nc.sync.dma_start(x_tile[:], x)
+        w_tile = held.tile([P, EXPERTS, P], BF16, name="w_tile")
+        nc.scalar.dma_start(w_tile[:], w.rearrange("e k m -> k e m"))
+        bias = held.tile([P, 1], F32, name="bias")
+        nc.gpsimd.dma_start(bias[:], b)
+
+        window = psum.tile([P, TOKENS], F32, name="window")
+        nc.tensor.matmul(window[:], ident[:], base_tile[:], start=True, stop=False)
+
+        for e in range(EXPERTS):
+            nc.tensor.matmul(
+                window[:].indirect(offsets[:, e * PIECE_COLS : (e + 1) * PIECE_COLS]),
+                w_tile[:, e, :],
+                x_tile[:, e * PIECE : (e + 1) * PIECE],
+                start=False,
+                stop=(e == EXPERTS - 1),
+            )
+
+        result = held.tile([P, TOKENS], F32, name="result")
+        nc.vector.tensor_scalar(result[:], window[:], bias[:, 0:1], 0.0, ADD, MAX)
+        nc.sync.dma_start(out, result[:])

@@ -24,14 +24,14 @@ def tile_scatter_matmul_kernel(tc, base, x, w, b, offs, out):
 
         offsets = held.tile([P, TOKENS // 16], U16, name="offsets")
         nc.sync.dma_start(offsets[:], offs)
-        base_tile = held.tile([P, TOKENS], BF16, name="base_tile")
-        nc.scalar.dma_start(base_tile[:], base)
-        x_tile = held.tile([P, TOKENS], BF16, name="x_tile")
-        nc.sync.dma_start(x_tile[:], x)
         w_tile = held.tile([P, EXPERTS, P], BF16, name="w_tile")
         nc.scalar.dma_start(w_tile[:], w.rearrange("e k m -> k e m"))
+        base_tile = held.tile([P, TOKENS], BF16, name="base_tile")
+        nc.sync.dma_start(base_tile[:], base)
         bias = held.tile([P, 1], F32, name="bias")
-        nc.gpsimd.dma_start(bias[:], b)
+        nc.scalar.dma_start(bias[:], b)
+        x_tile = held.tile([P, TOKENS], BF16, name="x_tile")
+        nc.sync.dma_start(x_tile[:], x)
 
         window = psum.tile([P, TOKENS], F32, name="window")
         nc.tensor.matmul(window[:], ident[:], base_tile[:], start=True, stop=False)

@@ -22,16 +22,18 @@ def tile_scatter_matmul_kernel(tc, base, x, w, b, offs, out):
         ident = held.tile([P, P], BF16, name="ident")
         make_identity(nc, ident[:])
 
+        queue_of = (nc.scalar, nc.sync)
         offsets = held.tile([P, TOKENS // 16], U16, name="offsets")
         nc.sync.dma_start(offsets[:], offs)
-        w_tile = held.tile([P, EXPERTS, P], BF16, name="w_tile")
-        nc.scalar.dma_start(w_tile[:], w.rearrange("e k m -> k e m"))
         base_tile = held.tile([P, TOKENS], BF16, name="base_tile")
-        nc.sync.dma_start(base_tile[:], base)
-        bias = held.tile([P, 1], F32, name="bias")
-        nc.scalar.dma_start(bias[:], b)
+        nc.scalar.dma_start(base_tile[:], base)
         x_tile = held.tile([P, TOKENS], BF16, name="x_tile")
         nc.sync.dma_start(x_tile[:], x)
+        w_tiles = [held.tile([P, P], BF16, name=f"w{e}") for e in range(EXPERTS)]
+        for e in range(EXPERTS):
+            queue_of[e % 2].dma_start(w_tiles[e][:], w[e])
+        bias = held.tile([P, 1], F32, name="bias")
+        nc.scalar.dma_start(bias[:], b)
 
         window = psum.tile([P, TOKENS], F32, name="window")
         nc.tensor.matmul(window[:], ident[:], base_tile[:], start=True, stop=False)
@@ -39,7 +41,7 @@ def tile_scatter_matmul_kernel(tc, base, x, w, b, offs, out):
         for e in range(EXPERTS):
             nc.tensor.matmul(
                 window[:].indirect(offsets[:, e * PIECE_COLS : (e + 1) * PIECE_COLS]),
-                w_tile[:, e, :],
+                w_tiles[e][:],
                 x_tile[:, e * PIECE : (e + 1) * PIECE],
                 start=False,
                 stop=(e == EXPERTS - 1),

@@ -22,16 +22,14 @@ def tile_scatter_matmul_kernel(tc, base, x, w, b, offs, out):
         ident = held.tile([P, P], BF16, name="ident")
         make_identity(nc, ident[:])
 
-        queue_of = (nc.scalar, nc.sync)
+        base_tile = held.tile([P, TOKENS], BF16, name="base_tile")
+        nc.sync.dma_start(base_tile[:], base)
+        w_tile = held.tile([P, EXPERTS, P], BF16, name="w_tile")
+        nc.scalar.dma_start(w_tile[:], w.rearrange("e k m -> k e m"))
         offsets = held.tile([P, TOKENS // 16], U16, name="offsets")
         nc.sync.dma_start(offsets[:], offs)
-        base_tile = held.tile([P, TOKENS], BF16, name="base_tile")
-        nc.scalar.dma_start(base_tile[:], base)
         x_tile = held.tile([P, TOKENS], BF16, name="x_tile")
-        nc.sync.dma_start(x_tile[:], x)
-        w_tiles = [held.tile([P, P], BF16, name=f"w{e}") for e in range(EXPERTS)]
-        for e in range(EXPERTS):
-            queue_of[e % 2].dma_start(w_tiles[e][:], w[e])
+        nc.scalar.dma_start(x_tile[:], x)
         bias = held.tile([P, 1], F32, name="bias")
         nc.scalar.dma_start(bias[:], b)
 
@@ -41,7 +39,7 @@ def tile_scatter_matmul_kernel(tc, base, x, w, b, offs, out):
         for e in range(EXPERTS):
             nc.tensor.matmul(
                 window[:].indirect(offsets[:, e * PIECE_COLS : (e + 1) * PIECE_COLS]),
-                w_tiles[e][:],
+                w_tile[:, e, :],
                 x_tile[:, e * PIECE : (e + 1) * PIECE],
                 start=False,
                 stop=(e == EXPERTS - 1),

@@ -4,6 +4,8 @@ from concourse.masks import make_identity
 P = 128
 TOKENS = 256
 EXPERTS = 4
+BANK = 512
+WARM_MATMULS = 2
 PIECE = 64
 PIECE_COLS = PIECE // 16
 
@@ -19,19 +21,25 @@ def tile_scatter_matmul_kernel(tc, base, x, w, b, offs, out):
         tc.tile_pool(name="held", bufs=1) as held,
         tc.psum_pool(name="psum", bufs=1) as psum,
     ):
+        zeros = held.tile([P, BANK], BF16, name="zeros")
+        nc.vector.memset(zeros[:], 0.0)
+        spare = psum.tile([P, BANK], F32, name="spare")
+        for _ in range(WARM_MATMULS):
+            nc.tensor.matmul(spare[:], zeros[:, 0:P], zeros[:], start=True, stop=True)
+
         ident = held.tile([P, P], BF16, name="ident")
         make_identity(nc, ident[:])
 
-        base_tile = held.tile([P, TOKENS], BF16, name="base_tile")
-        nc.sync.dma_start(base_tile[:], base)
-        w_tile = held.tile([P, EXPERTS, P], BF16, name="w_tile")
-        nc.scalar.dma_start(w_tile[:], w.rearrange("e k m -> k e m"))
         offsets = held.tile([P, TOKENS // 16], U16, name="offsets")
         nc.sync.dma_start(offsets[:], offs)
-        x_tile = held.tile([P, TOKENS], BF16, name="x_tile")
-        nc.scalar.dma_start(x_tile[:], x)
+        w_tile = held.tile([P, EXPERTS, P], BF16, name="w_tile")
+        nc.scalar.dma_start(w_tile[:], w.rearrange("e k m -> k e m"))
+        base_tile = held.tile([P, TOKENS], BF16, name="base_tile")
+        nc.sync.dma_start(base_tile[:], base)
         bias = held.tile([P, 1], F32, name="bias")
         nc.scalar.dma_start(bias[:], b)
+        x_tile = held.tile([P, TOKENS], BF16, name="x_tile")
+        nc.sync.dma_start(x_tile[:], x)
 
         window = psum.tile([P, TOKENS], F32, name="window")
         nc.tensor.matmul(window[:], ident[:], base_tile[:], start=True, stop=False)

@@ -24,22 +24,22 @@ def tile_scatter_matmul_kernel(tc, base, x, w, b, offs, out):
         zeros = held.tile([P, BANK], BF16, name="zeros")
         nc.vector.memset(zeros[:], 0.0)
         spare = psum.tile([P, BANK], F32, name="spare")
-        for _ in range(WARM_MATMULS):
+        for repeat in range(WARM_MATMULS):
             nc.tensor.matmul(spare[:], zeros[:, 0:P], zeros[:], start=True, stop=True)
 
         ident = held.tile([P, P], BF16, name="ident")
         make_identity(nc, ident[:])
 
-        offsets = held.tile([P, TOKENS // 16], U16, name="offsets")
-        nc.sync.dma_start(offsets[:], offs)
-        w_tile = held.tile([P, EXPERTS, P], BF16, name="w_tile")
-        nc.scalar.dma_start(w_tile[:], w.rearrange("e k m -> k e m"))
         base_tile = held.tile([P, TOKENS], BF16, name="base_tile")
         nc.sync.dma_start(base_tile[:], base)
-        bias = held.tile([P, 1], F32, name="bias")
-        nc.scalar.dma_start(bias[:], b)
+        offsets = held.tile([P, TOKENS // 16], U16, name="offsets")
+        nc.sync.dma_start(offsets[:], offs)
         x_tile = held.tile([P, TOKENS], BF16, name="x_tile")
         nc.sync.dma_start(x_tile[:], x)
+        w_tile = held.tile([P, EXPERTS, P], BF16, name="w_tile")
+        nc.sync.dma_start(w_tile[:], w.rearrange("e k m -> k e m"))
+        bias = held.tile([P, 1], F32, name="bias")
+        nc.sync.dma_start(bias[:], b)
 
         window = psum.tile([P, TOKENS], F32, name="window")
         nc.tensor.matmul(window[:], ident[:], base_tile[:], start=True, stop=False)

@@ -4,6 +4,7 @@ from concourse.masks import make_identity
 P = 128
 TOKENS = 256
 EXPERTS = 4
+HALF = 2
 BANK = 512
 WARM_MATMULS = 2
 PIECE = 64
@@ -36,8 +37,13 @@ def tile_scatter_matmul_kernel(tc, base, x, w, b, offs, out):
         nc.sync.dma_start(offsets[:], offs)
         x_tile = held.tile([P, TOKENS], BF16, name="x_tile")
         nc.sync.dma_start(x_tile[:], x)
-        w_tile = held.tile([P, EXPERTS, P], BF16, name="w_tile")
-        nc.sync.dma_start(w_tile[:], w.rearrange("e k m -> k e m"))
+        w_tiles = []
+        for half in range(EXPERTS // HALF):
+            w_tile = held.tile([P, HALF, P], BF16, name="w_tile%d" % half)
+            nc.sync.dma_start(
+                w_tile[:], w[half * HALF : (half + 1) * HALF].rearrange("e k m -> k e m")
+            )
+            w_tiles.append(w_tile)
         bias = held.tile([P, 1], F32, name="bias")
         nc.sync.dma_start(bias[:], b)
 
@@ -47,7 +53,7 @@ def tile_scatter_matmul_kernel(tc, base, x, w, b, offs, out):
         for e in range(EXPERTS):
             nc.tensor.matmul(
                 window[:].indirect(offsets[:, e * PIECE_COLS : (e + 1) * PIECE_COLS]),
-                w_tile[:, e, :],
+                w_tiles[e // HALF][:, e % HALF, :],
                 x_tile[:, e * PIECE : (e + 1) * PIECE],
                 start=False,
                 stop=(e == EXPERTS - 1),

@@ -7,6 +7,7 @@ EXPERTS = 4
 HALF = 2
 BANK = 512
 WARM_MATMULS = 2
+BLOCK = 32
 PIECE = 64
 PIECE_COLS = PIECE // 16
 
@@ -22,6 +23,10 @@ def tile_scatter_matmul_kernel(tc, base, x, w, b, offs, out):
         tc.tile_pool(name="held", bufs=1) as held,
         tc.psum_pool(name="psum", bufs=1) as psum,
     ):
+        bias_rows = held.tile([P, BLOCK], F32, name="bias_rows", align_bytes=64)
+        nc.vector.memset(bias_rows[:], 0.0)
+        nc.scalar.dma_start(bias_rows[0:P:BLOCK, :], b.rearrange("(q j) o -> q (o j)", j=BLOCK))
+
         zeros = held.tile([P, BANK], BF16, name="zeros")
         nc.vector.memset(zeros[:], 0.0)
         spare = psum.tile([P, BANK], F32, name="spare")
@@ -44,8 +49,8 @@ def tile_scatter_matmul_kernel(tc, base, x, w, b, offs, out):
                 w_tile[:], w[half * HALF : (half + 1) * HALF].rearrange("e k m -> k e m")
             )
             w_tiles.append(w_tile)
-        bias = held.tile([P, 1], F32, name="bias")
-        nc.sync.dma_start(bias[:], b)
+        bias_columns = held.tile([P, BLOCK], F32, name="bias_columns", align_bytes=64)
+        nc.vector.transpose(bias_columns[:], bias_rows[:])
 
         window = psum.tile([P, TOKENS], F32, name="window")
         nc.tensor.matmul(window[:], ident[:], base_tile[:], start=True, stop=False)
@@ -60,5 +65,5 @@ def tile_scatter_matmul_kernel(tc, base, x, w, b, offs, out):
             )
 
         result = held.tile([P, TOKENS], F32, name="result")
-        nc.vector.tensor_scalar(result[:], window[:], bias[:, 0:1], 0.0, ADD, MAX)
+        nc.vector.tensor_scalar(result[:], window[:], bias_columns[:, 0:1], 0.0, ADD, MAX)
         nc.sync.dma_start(out, result[:])

@@ -25,7 +25,6 @@ def tile_scatter_matmul_kernel(tc, base, x, w, b, offs, out):
     ):
         bias_rows = held.tile([P, BLOCK], F32, name="bias_rows", align_bytes=64)
         nc.vector.memset(bias_rows[:], 0.0)
-        nc.scalar.dma_start(bias_rows[0:P:BLOCK, :], b.rearrange("(q j) o -> q (o j)", j=BLOCK))
 
         zeros = held.tile([P, BANK], BF16, name="zeros")
         nc.vector.memset(zeros[:], 0.0)
@@ -49,6 +48,7 @@ def tile_scatter_matmul_kernel(tc, base, x, w, b, offs, out):
                 w_tile[:], w[half * HALF : (half + 1) * HALF].rearrange("e k m -> k e m")
             )
             w_tiles.append(w_tile)
+        nc.sync.dma_start(bias_rows[0:P:BLOCK, :], b.rearrange("(q j) o -> q (o j)", j=BLOCK))
         bias_columns = held.tile([P, BLOCK], F32, name="bias_columns", align_bytes=64)
         nc.vector.transpose(bias_columns[:], bias_rows[:])
 

@@ -5,8 +5,7 @@ P = 128
 TOKENS = 256
 EXPERTS = 4
 HALF = 2
-BANK = 512
-WARM_MATMULS = 2
+WARM_MATMULS = 8
 BLOCK = 32
 PIECE = 64
 PIECE_COLS = PIECE // 16
@@ -24,13 +23,13 @@ def tile_scatter_matmul_kernel(tc, base, x, w, b, offs, out):
         tc.psum_pool(name="psum", bufs=1) as psum,
     ):
         bias_rows = held.tile([P, BLOCK], F32, name="bias_rows", align_bytes=64)
-        nc.vector.memset(bias_rows[:], 0.0)
 
-        zeros = held.tile([P, BANK], BF16, name="zeros")
+        zeros = held.tile([P, P], BF16, name="zeros")
         nc.vector.memset(zeros[:], 0.0)
-        spare = psum.tile([P, BANK], F32, name="spare")
+        nc.vector.memset(bias_rows[:], 0.0)
+        spare = psum.tile([P, P], F32, name="spare")
         for repeat in range(WARM_MATMULS):
-            nc.tensor.matmul(spare[:], zeros[:, 0:P], zeros[:], start=True, stop=True)
+            nc.tensor.matmul(spare[:], zeros[:], zeros[:], start=True, stop=True)
 
         ident = held.tile([P, P], BF16, name="ident")
         make_identity(nc, ident[:])

@@ -1,5 +1,4 @@
 import concourse.mybir as mybir
-from concourse.masks import make_identity
 
 P = 128
 TOKENS = 256
@@ -12,6 +11,7 @@ PIECE_COLS = PIECE // 16
 
 BF16, F32, U16 = mybir.dt.bfloat16, mybir.dt.float32, mybir.dt.uint16
 ADD, MAX = mybir.AluOpType.add, mybir.AluOpType.max
+MULT, IS_EQUAL = mybir.AluOpType.mult, mybir.AluOpType.is_equal
 
 FLOPS = 2 * P * P * TOKENS
 
@@ -31,8 +31,17 @@ def tile_scatter_matmul_kernel(tc, base, x, w, b, offs, out):
         for repeat in range(WARM_MATMULS):
             nc.tensor.matmul(spare[:], zeros[:], zeros[:], start=True, stop=True)
 
+        ones = held.tile([P, BLOCK], F32, name="ones")
+        nc.vector.memset(ones[:], 1.0)
         ident = held.tile([P, P], BF16, name="ident")
-        make_identity(nc, ident[:])
+        nc.vector.memset(ident[:], 0.0)
+        ramp = held.tile([P, BLOCK], F32, name="ramp", align_bytes=64)
+        nc.vector.tensor_tensor_scan(ramp[:], ones[:], ones[:], -1.0, MULT, ADD)
+        place = held.tile([P, BLOCK], F32, name="place", align_bytes=64)
+        nc.vector.transpose(place[:], ramp[:])
+        for start in range(0, P, BLOCK):
+            block = slice(start, start + BLOCK)
+            nc.vector.tensor_tensor(ident[block, block], ramp[block, :], place[block, :], IS_EQUAL)
 
         base_tile = held.tile([P, TOKENS], BF16, name="base_tile")
         nc.sync.dma_start(base_tile[:], base)

import concourse.mybir as mybir

P = 128
TOKENS = 256
EXPERTS = 4
HALF = 2
WARM_MATMULS = 8
BLOCK = 32
PIECE = 64
PIECE_COLS = PIECE // 16

BF16, F32, U16 = mybir.dt.bfloat16, mybir.dt.float32, mybir.dt.uint16
ADD, MAX = mybir.AluOpType.add, mybir.AluOpType.max
MULT, IS_EQUAL = mybir.AluOpType.mult, mybir.AluOpType.is_equal

FLOPS = 2 * P * P * TOKENS


def tile_scatter_matmul_kernel(tc, base, x, w, b, offs, out):
    nc = tc.nc
    with (
        tc.tile_pool(name="held", bufs=1) as held,
        tc.psum_pool(name="psum", bufs=1) as psum,
    ):
        bias_rows = held.tile([P, BLOCK], F32, name="bias_rows", align_bytes=64)

        zeros = held.tile([P, P], BF16, name="zeros")
        nc.vector.memset(zeros[:], 0.0)
        nc.vector.memset(bias_rows[:], 0.0)
        spare = psum.tile([P, P], F32, name="spare")
        for repeat in range(WARM_MATMULS):
            nc.tensor.matmul(spare[:], zeros[:], zeros[:], start=True, stop=True)

        ones = held.tile([P, BLOCK], F32, name="ones")
        nc.vector.memset(ones[:], 1.0)
        ident = held.tile([P, P], BF16, name="ident")
        nc.vector.memset(ident[:], 0.0)
        ramp = held.tile([P, BLOCK], F32, name="ramp", align_bytes=64)
        nc.vector.tensor_tensor_scan(ramp[:], ones[:], ones[:], -1.0, MULT, ADD)
        place = held.tile([P, BLOCK], F32, name="place", align_bytes=64)
        nc.vector.transpose(place[:], ramp[:])
        for start in range(0, P, BLOCK):
            block = slice(start, start + BLOCK)
            nc.vector.tensor_tensor(ident[block, block], ramp[block, :], place[block, :], IS_EQUAL)

        base_tile = held.tile([P, TOKENS], BF16, name="base_tile")
        nc.sync.dma_start(base_tile[:], base)
        offsets = held.tile([P, TOKENS // 16], U16, name="offsets")
        nc.sync.dma_start(offsets[:], offs)
        x_tile = held.tile([P, TOKENS], BF16, name="x_tile")
        nc.sync.dma_start(x_tile[:], x)
        w_tiles = []
        for half in range(EXPERTS // HALF):
            w_tile = held.tile([P, HALF, P], BF16, name="w_tile%d" % half)
            nc.sync.dma_start(
                w_tile[:], w[half * HALF : (half + 1) * HALF].rearrange("e k m -> k e m")
            )
            w_tiles.append(w_tile)
        nc.sync.dma_start(bias_rows[0:P:BLOCK, :], b.rearrange("(q j) o -> q (o j)", j=BLOCK))
        bias_columns = held.tile([P, BLOCK], F32, name="bias_columns", align_bytes=64)
        nc.vector.transpose(bias_columns[:], bias_rows[:])

        window = psum.tile([P, TOKENS], F32, name="window")
        nc.tensor.matmul(window[:], ident[:], base_tile[:], start=True, stop=False)

        for e in range(EXPERTS):
            nc.tensor.matmul(
                window[:].indirect(offsets[:, e * PIECE_COLS : (e + 1) * PIECE_COLS]),
                w_tiles[e // HALF][:, e % HALF, :],
                x_tile[:, e * PIECE : (e + 1) * PIECE],
                start=False,
                stop=(e == EXPERTS - 1),
            )

        result = held.tile([P, TOKENS], F32, name="result")
        nc.vector.tensor_scalar(result[:], window[:], bias_columns[:, 0:1], 0.0, ADD, MAX)
        nc.sync.dma_start(out, result[:])
